import numpy as np
import ml_dtypes


def mxq(x, axis, fmt="e4m3"):
    dtype, down = {"e4m3": (ml_dtypes.float8_e4m3fn, 7), "e5m2": (ml_dtypes.float8_e5m2, 14)}[fmt]
    v = np.moveaxis(np.asarray(x, np.float32).astype(ml_dtypes.bfloat16).astype(np.float64), axis, -1)
    blocks = v.reshape(v.shape[:-1] + (-1, 32))
    amax = np.abs(blocks).max(-1, keepdims=True)
    byte = np.maximum(np.where(amax > 0, np.frexp(amax)[1] - 1 + 127, 0) - down, 1)
    scale = np.exp2(byte - 127.0)
    codes = (blocks / scale).astype(np.float32).astype(dtype).astype(np.float64)
    return np.moveaxis((codes * scale).reshape(v.shape), -1, axis)


WIDE = False


def mx_kscale(k):
    if not WIDE:
        return np.ones(k)
    levels = np.array([10, -10, 5, -5, 0])
    if k % 512:
        return np.exp2(np.random.permutation(np.resize(levels, k // 32))).repeat(32)
    a = np.empty((k // 512, 16))
    for p in range(k // 512):
        a[p, :8] = np.random.permutation(np.resize(levels, 8))
        for g in range(8):
            far = levels[np.abs(levels - a[p, g]) >= 10]
            a[p, g + 8] = far[np.random.randint(len(far))]
    return np.exp2(a.ravel()).repeat(32)


def f64(x):
    return np.asarray(x).astype(np.float64)


def striped(idx):
    return np.tile(idx.reshape(-1, 16).T, (8, 1)).astype(np.uint16)


def unstriped(offs):
    return offs[:16].T.reshape(-1).astype(np.int64)


E2M1 = np.array([0.0, 0.5, 1.0, 1.5, 2.0, 3.0, 4.0, 6.0, -0.0, -0.5, -1.0, -1.5, -2.0, -3.0, -4.0, -6.0])


def pack_weight(w, fmt):
    k, n = w.shape
    w = f64(np.asarray(w, np.float32).astype(ml_dtypes.bfloat16)).reshape(k // 32, 32, n)
    amax = np.abs(w).max(1)
    if fmt == "e4m3":
        byte = np.frexp(amax)[1] - 1 + 127 - 7
    else:
        mant, ex = np.frexp(amax / 6.0)
        byte = np.where(mant > 0.5, ex, ex - 1) + 127
    byte = np.clip(np.where(amax > 0, byte, 1), 1, 254)
    scaled = (w * np.exp2(127.0 - byte)[:, None, :]).reshape(k, n).astype(np.float32)
    by_word = np.ascontiguousarray(scaled.reshape(k // 512, 128, 4, n).transpose(0, 1, 3, 2))
    if fmt == "e4m3":
        words = by_word.astype(ml_dtypes.float8_e4m3fn).view(np.uint8)
    else:
        c = by_word.astype(ml_dtypes.float4_e2m1fn).view(np.uint8) & 0xF
        words = (c[..., 0::2] | (c[..., 1::2] << 4)).reshape(k // 512, 128, 2 * n)
    return np.ascontiguousarray(words), np.ascontiguousarray(byte.astype(np.uint8).reshape(k // 512, 16, n))


def unpack_weight(words, scales, fmt):
    g, _, n = scales.shape
    words = np.ascontiguousarray(words).reshape(g, 128, n, -1)
    if fmt == "e4m3":
        vals = words.view(ml_dtypes.float8_e4m3fn).astype(np.float64)
    else:
        nib = np.empty((g, 128, n, 4), np.uint8)
        nib[..., 0::2] = words & 0xF
        nib[..., 1::2] = words >> 4
        vals = E2M1[nib]
    vals = vals * np.repeat(np.exp2(scales.astype(np.float64) - 127.0), 8, axis=1)[..., None]
    return vals.transpose(0, 1, 3, 2).reshape(g * 512, n)


def gelu(v):
    return 0.5 * v * (1.0 + np.tanh(np.sqrt(2.0 / np.pi) * (v + 0.044715 * v**3)))


def bf(x):
    return np.asarray(x, np.float32).astype(ml_dtypes.bfloat16)


def planes(Y):
    n, m = Y.shape
    b = f64(bf(Y)).reshape(n // 32, 32, m)
    amax = np.abs(b).max(1)
    byte = np.clip(np.where(amax > 0, np.frexp(amax)[1] - 1 + 127 - 7, 1), 1, 254)
    codes = (b * np.exp2(127.0 - byte)[:, None, :]).reshape(n, m).astype(np.float32).astype(ml_dtypes.float8_e4m3fn).view(np.uint8)
    words = codes.reshape(n // 512, 128, 4, m).transpose(0, 1, 3, 2)
    return np.ascontiguousarray(words), np.ascontiguousarray(byte.astype(np.uint8).reshape(n // 512, 16, m))


K, T, S, H, N, P = 1024, 2048, 1024, 512, 1024, 512

def setup_inputs():
    n = np.random.standard_normal
    s = mx_kscale(K)[:, None]
    u = mx_kscale(H)[:, None]
    d = {}
    d["tab_words"], d["tab_scales"] = pack_weight(n((K, T)) * s, "e4m3")
    d["offs"] = striped(np.random.permutation(T)[:S])
    order = np.random.permutation(S)
    d["pos1"] = striped(order[:P])
    d["pos2"] = striped(order[P:])
    d["w1"] = (0.52 * n((K, H)) / np.sqrt(K) / s).astype(np.float32)
    d["w2_words"], d["w2_scales"] = pack_weight(0.52 * n((K, H)) / np.sqrt(K) / s, "e4m3")
    d["soft"] = (0.6 * np.exp(0.3 * n(H))).astype(np.float32)
    d["gain"] = (np.exp(0.3 * n(H)) * u[:, 0]).astype(np.float32)
    w4 = n((H, N)) / np.sqrt(H) / u * np.exp(0.8 * n(N))
    d["w4_words"], d["w4_scales"] = pack_weight(w4, "e2m1")
    d["field"] = np.exp(0.4 * n((N, S))).astype(np.float32)
    return d

def reference(tab_words, tab_scales, offs, pos1, pos2, w1, w2_words, w2_scales, soft, gain, w4_words, w4_scales, field):
    v = unpack_weight(tab_words, tab_scales, "e4m3")[:, unstriped(offs)]
    a = mxq(f64(w1), 0, "e4m3").T @ v
    b = unpack_weight(w2_words, w2_scales, "e4m3").T @ v
    h = (np.cos(a) * f64(soft)[:, None] - np.sin(b)) * f64(gain)[:, None]
    hq = mxq(h, 0, "e4m3")
    g2 = (unpack_weight(w4_words, w4_scales, "e2m1").T @ hq) * f64(field)
    y = np.maximum(g2[:, unstriped(pos1)], g2[:, unstriped(pos2)])
    words, scales = planes(y)
    return y, words, scales

@@ -1,0 +1,288 @@
+import math
+from contextlib import ExitStack
+
+import concourse.mybir as mybir
+
+K, T, S, H, N, PAIRS = 1024, 2048, 1024, 512, 1024, 512
+FLOPS = 2 * (2 * K * H * S + H * N * S)
+
+F32 = mybir.dt.float32
+BF16 = mybir.dt.bfloat16
+I32 = mybir.dt.int32
+U32 = mybir.dt.uint32
+U16 = mybir.dt.uint16
+U8 = mybir.dt.uint8
+FP8X4 = mybir.dt.float8_e4m3fn_x4
+FP4X4 = mybir.dt.float4_e2m1fn_x4
+ALU = mybir.AluOpType
+ACT = mybir.ActivationFunctionType
+
+P = 128
+PACK = 4
+PASSES = K // (P * PACK)
+GROUPS = N // (P * PACK)
+QUADS = 4
+CHUNKS = (512, 256, 256)
+
+
+def tile_list_compass_deviation_card_kernel(
+    tc, tab_words, tab_scales, offs, pos1, pos2, w1, w2_words, w2_scales, soft, gain,
+    w4_words, w4_scales, field, out_0, out_1, out_2,
+):
+    nc = tc.nc
+    with ExitStack() as ctx:
+        keep = ctx.enter_context(tc.tile_pool(name="keep", bufs=1))
+        work = ctx.enter_context(tc.tile_pool(name="work", bufs=2))
+        psum = ctx.enter_context(tc.psum_pool(name="psum", bufs=4))
+
+        def load_scale_rows(queue, tile, scales):
+            planes = scales.shape[0]
+            for q in range(QUADS):
+                queue.dma_start(
+                    out=tile[32 * q : 32 * q + 4 * planes, :].bitcast(I32),
+                    in_=scales.bitcast(I32)[:, 4 * q : 4 * q + 4, :],
+                )
+
+        stage = ctx.enter_context(tc.tile_pool(name="stage", bufs=1))
+        ROOM = 8192
+        tab_s = keep.tile([P, T], U8, name="tab_s", align_bytes=64)
+        nc.gpsimd.memset(tab_s[:].bitcast(I32), 0)
+        one = stage.tile([P, ROOM], F32, name="one", offset=ROOM)
+        nc.gpsimd.memset(one[:, 0:1], 1.0)
+        half_pi = keep.tile([P, 1], F32, name="half_pi")
+        nc.vector.tensor_scalar(out=half_pi[:], in0=one[:, 0:1], scalar1=math.pi / 2, scalar2=None, op0=ALU.mult)
+        w2_s_raw = stage.tile([P, H], U8, name="w2_s_raw", offset=4 * ROOM + 6144 + 64)
+        nc.gpsimd.memset(w2_s_raw[:].bitcast(I32), 0)
+        w4_s_raw = stage.tile([P, N], U8, name="w4_s_raw", offset=4 * ROOM + 6144 + 576)
+        nc.gpsimd.memset(w4_s_raw[:].bitcast(I32), 0)
+
+        tab_w = [stage.tile([P, T], I32, name=f"tab_w{a}", offset=a * ROOM) for a in range(PASSES)]
+        w1_raw = [stage.tile([P, PACK, H], F32, name=f"w1_raw{a}", offset=(2 + a) * ROOM) for a in range(PASSES)]
+        w2_raw = stage.tile([P, PASSES, H], I32, name="w2_raw", offset=4 * ROOM)
+        w4_raw = stage.tile([P, N // 2], I32, name="w4_raw", offset=4 * ROOM + 4096)
+        soft_sb = stage.tile([P, PACK], F32, name="soft_sb", offset=4 * ROOM + 6144)
+        gain_sb = stage.tile([P, PACK], F32, name="gain_sb", offset=4 * ROOM + 6144 + 32)
+
+        def load_tab(a):
+            nc.sync.dma_start(out=tab_w[a][:], in_=tab_words[a].rearrange("p t i -> p (t i)").bitcast(I32))
+
+        def load_w1(a):
+            nc.sync.dma_start(
+                out=w1_raw[a][:], in_=w1[512 * a : 512 * (a + 1), :].rearrange("(p i) r -> p i r", i=PACK)
+            )
+
+        offs_sb = keep.tile([P, S // 16], U16, name="offs_sb")
+        nc.sync.dma_start(out=offs_sb[:], in_=offs)
+        load_tab(0)
+        pos1_sb = keep.tile([P, PAIRS // 16], U16, name="pos1_sb")
+        nc.sync.dma_start(out=pos1_sb[:], in_=pos1)
+        pos2_sb = keep.tile([P, PAIRS // 16], U16, name="pos2_sb")
+        nc.sync.dma_start(out=pos2_sb[:], in_=pos2)
+        load_scale_rows(nc.scalar, tab_s, tab_scales)
+        load_w1(0)
+        load_w1(1)
+        load_tab(1)
+        nc.sync.dma_start(out=w2_raw[:], in_=w2_words.rearrange("a p c i -> p a (c i)").bitcast(I32))
+        load_scale_rows(nc.sync, w2_s_raw, w2_scales)
+        nc.sync.dma_start(out=soft_sb[:], in_=soft.rearrange("(p t) -> p t", t=PACK))
+        nc.sync.dma_start(out=gain_sb[:], in_=gain.rearrange("(p t) -> p t", t=PACK))
+        nc.sync.dma_start(out=w4_raw[:], in_=w4_words[0].bitcast(I32))
+        load_scale_rows(nc.sync, w4_s_raw, w4_scales)
+
+        starts = [sum(CHUNKS[:c]) for c in range(len(CHUNKS))]
+        v_s, v_w = {}, {}
+
+        def entries(c):
+            return offs_sb[:, starts[c] // 16 : (starts[c] + CHUNKS[c]) // 16]
+
+        def gather_words(a, c):
+            if a == 0:
+                vw = keep.tile([P, CHUNKS[c]], U32, name=f"v_w{a}{c}", align_bytes=64)
+            else:
+                vw = stage.tile(
+                    [P, CHUNKS[c]], U32, name=f"v_w{a}{c}", align_bytes=64, offset=5 * ROOM + 4096 + 4 * starts[c]
+                )
+            nc.vector.tensor_copy(out=vw[:], in_=tab_w[a][:].bitcast(U32).indirect(entries(c)))
+            v_w[a, c] = vw[:]
+
+        def gather_scales(c):
+            vs = keep.tile([P, CHUNKS[c]], U8, name=f"v_s{c}", align_bytes=64)
+            nc.vector.tensor_copy(out=vs[:], in_=tab_s[:].indirect(entries(c)))
+            v_s[c] = vs
+
+        for c in range(len(CHUNKS)):
+            gather_scales(c)
+        for c in range(len(CHUNKS)):
+            gather_words(0, c)
+
+        w1_w, w1_s = [], []
+        for a in range(PASSES):
+            if a == 0:
+                wb = keep.tile([P, H * PACK], BF16, name=f"w1_bf{a}", align_bytes=64)
+            else:
+                wb = stage.tile([P, H * PACK], BF16, name=f"w1_bf{a}", align_bytes=64, offset=5 * ROOM + 4096 - 64)
+            for ms, copy in ((slice(0, P // 2), nc.scalar.copy), (slice(P // 2, P), nc.vector.tensor_copy)):
+                copy(
+                    out=wb[:].rearrange("p (t m i) -> p m i t", t=PACK, i=PACK)[:, ms],
+                    in_=w1_raw[a][:].rearrange("p i (m t) -> p m i t", t=PACK)[:, ms],
+                )
+            ww = keep.tile([P, H], U32, name=f"w1_w{a}", align_bytes=64)
+            ws = keep.tile([P, H], U8, name=f"w1_s{a}", align_bytes=64)
+            nc.vector.quantize_mx(out=ww[:].bitcast(FP8X4), scales=ws[:], in_=wb[:])
+            w1_w.append(ww)
+            w1_s.append(ws)
+
+        gather_words(1, 0)
+
+        w2_w = stage.tile([P, PASSES, H], I32, name="w2_w", align_bytes=64, offset=5 * ROOM)
+        nc.vector.tensor_copy(
+            out=w2_w[:].rearrange("p a (t m e) -> p a m t e", t=PACK, e=4),
+            in_=w2_raw[:].rearrange("p a (m e t) -> p a m t e", t=PACK, e=4),
+        )
+        w2_s = stage.tile([P, H], U8, name="w2_s", align_bytes=64, offset=4 * ROOM + 3072)
+        nc.vector.tensor_copy(
+            out=w2_s[:].rearrange("p (t m) -> p t m", t=PACK),
+            in_=w2_s_raw[:].rearrange("p (m t) -> p t m", t=PACK),
+        )
+        for c in range(1, len(CHUNKS)):
+            gather_words(1, c)
+
+        field_rows = field.rearrange("(g p u t) j -> g u p t j", p=P, u=2, t=2)
+        field_sb = {}
+        for k, room in enumerate((0, 2, 3, 1)):
+            g, pair = divmod(k, 2)
+            f = stage.tile([P, 2, S], F32, name=f"field{k}", offset=room * ROOM)
+            nc.sync.dma_start(out=f[:], in_=field_rows[g, pair])
+            for t in range(2):
+                field_sb[g, 2 * pair + t] = f[:, t, :]
+
+        w4_w = stage.tile([P, N // 2], I32, name="w4_w", align_bytes=64, offset=4 * ROOM)
+        nc.vector.tensor_copy(
+            out=w4_w[:].bitcast(U16).rearrange("p (g t m) -> p g t m", g=GROUPS, t=PACK),
+            in_=w4_raw[:].bitcast(U16).rearrange("p (g m t) -> p g t m", g=GROUPS, t=PACK),
+        )
+        w4_s = stage.tile([P, N], U8, name="w4_s", align_bytes=64, offset=4 * ROOM + 2048)
+        nc.vector.tensor_copy(
+            out=w4_s[:].rearrange("p (g t m) -> p g t m", g=GROUPS, t=PACK),
+            in_=w4_s_raw[:].rearrange("p (g m t) -> p g t m", g=GROUPS, t=PACK),
+        )
+
+        g2 = {}
+
+        h_q = []
+        def product(c, t, words, scales):
+            cols = slice(P * t, P * (t + 1))
+            acc = psum.tile([P, CHUNKS[c]], F32, name="first")
+            for a in range(PASSES):
+                nc.tensor.matmul_mx(
+                    out=acc[:],
+                    lhsT=words[a][:, cols].bitcast(FP8X4), lhsT_scale=scales[a][:, cols],
+                    rhs=v_w[a, c].bitcast(FP8X4), rhs_scale=v_s[c][4 * a : P, :],
+                    start=(a == 0), stop=(a == PASSES - 1),
+                )
+            return acc
+
+        def cosine(c, t):
+            acc = product(c, t, w1_w, w1_s)
+            abs_a = work.tile([P, CHUNKS[c]], F32, name="abs_a")
+            nc.scalar.activation(out=abs_a[:], in_=acc[:], func=ACT.Abs)
+            cos_a = work.tile([P, CHUNKS[c]], F32, name="cos_a", bufs=4)
+            nc.scalar.activation(out=cos_a[:], in_=abs_a[:], func=ACT.Sin, bias=half_pi[:], scale=-1.0)
+            return cos_a
+
+        def sine(c, t):
+            acc = product(c, t, [w2_w[:, a, :] for a in range(PASSES)], [w2_s[4 * a : P, :] for a in range(PASSES)])
+            sin_b = work.tile([P, CHUNKS[c]], F32, name="sin_b", bufs=4)
+            nc.scalar.activation(out=sin_b[:], in_=acc[:], func=ACT.Sin)
+            return sin_b
+
+        for c, width in enumerate(CHUNKS):
+            u = work.tile([P, PACK, width], F32, name="u")
+            if c == 0:
+                early = [cosine(c, t) for t in range(PACK)]
+            for t in range(PACK):
+                cos_a = early[t] if c == 0 else cosine(c, t)
+                sin_b = sine(c, t)
+                nc.vector.scalar_tensor_tensor(
+                    out=u[:, t, :], in0=cos_a[:], scalar=soft_sb[:, t : t + 1], in1=sin_b[:],
+                    op0=ALU.mult, op1=ALU.subtract,
+                )
+            h_bf = work.tile([P, width, PACK], BF16, name="h_bf", align_bytes=64)
+            nc.vector.tensor_tensor(
+                out=h_bf[:].rearrange("p (c e) t -> p c t e", e=4),
+                in0=u[:].rearrange("p t (c e) -> p c t e", e=4),
+                in1=gain_sb[:].unsqueeze(1).unsqueeze(3).to_broadcast([P, width // 4, PACK, 4]),
+                op=ALU.mult,
+            )
+            h_w = keep.tile([P, width], U32, name=f"h_w{c}", align_bytes=64)
+            h_s = keep.tile([P, width], U8, name=f"h_s{c}", align_bytes=64)
+            nc.vector.quantize_mx(out=h_w[:].bitcast(FP8X4), scales=h_s[:], in_=h_bf[:].rearrange("p j t -> p (j t)"))
+            h_q.append((h_w, h_s))
+
+        out_rows = out_0.rearrange("(g p t) m -> g t p m", p=P, t=PACK)
+        out_words = out_1.rearrange("g p m t -> g p (m t)").bitcast(I32)
+        y_s = keep.tile([P, PAIRS], U8, name="y_s", align_bytes=64)
+
+        def second_stage(g, t):
+            s = PACK * g + t
+            g2[g, t] = keep.tile([P, S], F32, name=f"g2_{s}", tag=f"ring{s % 3}")
+            if s >= 1:
+                sums = work.tile([P, S], F32, name="sums")
+            for c, width in enumerate(CHUNKS):
+                js = slice(starts[c], starts[c] + width)
+                acc = psum.tile([P, width], F32, name=f"second{min(c, 1)}", bufs=2)
+                nc.tensor.matmul_mx(
+                    out=acc[:],
+                    lhsT=w4_w[:].bitcast(U8)[:, 2 * P * s : 2 * P * (s + 1)].bitcast(FP4X4),
+                    lhsT_scale=w4_s[:, P * s : P * (s + 1)],
+                    rhs=h_q[c][0][:].bitcast(FP8X4), rhs_scale=h_q[c][1][:],
+                    start=True, stop=True,
+                )
+                if s >= 1:
+                    nc.scalar.copy(out=sums[:, js], in_=acc[:])
+                else:
+                    nc.vector.tensor_tensor(out=g2[g, t][:, js], in0=acc[:], in1=field_sb[g, t][:, js], op=ALU.mult)
+            if s >= 1:
+                nc.gpsimd.tensor_tensor(out=g2[g, t][:], in0=sums[:], in1=field_sb[g, t], op=ALU.mult)
+
+        def pick(g, t, y, ms, x):
+            cols = slice(ms.start // 16, ms.stop // 16)
+            nc.vector.tensor_copy(out=x[:, 0, ms], in_=g2[g, t][:].indirect(pos1_sb[:, cols]))
+            nc.vector.tensor_copy(out=x[:, 1, ms], in_=g2[g, t][:].indirect(pos2_sb[:, cols]))
+            nc.vector.tensor_tensor(out=y[:, t, ms], in0=x[:, 0, ms], in1=x[:, 1, ms], op=ALU.max)
+            nc.sync.dma_start(out=out_rows[g, t][:, ms], in_=y[:, t, ms])
+
+        def planes(g, y, ms, copy):
+            width = ms.stop - ms.start
+            y_bf = work.tile([P, width, PACK], BF16, name="y_bf", align_bytes=64)
+            copy(
+                out=y_bf[:].rearrange("p (c e) t -> p c t e", e=4),
+                in_=y[:, :, ms].rearrange("p t (c e) -> p c t e", e=4),
+            )
+            y_w = work.tile([P, width], I32, name="y_w", align_bytes=64)
+            nc.vector.quantize_mx(
+                out=y_w[:].bitcast(FP8X4), scales=y_s[4 * g : P, ms], in_=y_bf[:].rearrange("p m t -> p (m t)")
+            )
+            nc.sync.dma_start(out=out_words[g][:, ms], in_=y_w[:])
+
+        whole = slice(0, PAIRS)
+        halves = (slice(0, PAIRS // 2), slice(PAIRS // 2, PAIRS))
+        ys = [keep.tile([P, PACK, PAIRS], F32, name=f"y{g}") for g in range(GROUPS)]
+        slices = [(g, t) for g in range(GROUPS) for t in range(PACK)]
+        second_stage(*slices[0])
+        second_stage(*slices[1])
+        for i, (g, t) in enumerate(slices):
+            x = keep.tile([P, 2, PAIRS], F32, name=f"x{i}", tag=f"ring{(i + 2) % 3}")
+            for ms in (halves if i == len(slices) - 1 else (whole,)):
+                pick(g, t, ys[g], ms, x)
+            if (g, t) == (1, 0):
+                planes(0, ys[0], whole, nc.scalar.copy)
+            if i + 2 < len(slices):
+                second_stage(*slices[i + 2])
+        planes(g, ys[g], halves[0], nc.scalar.copy)
+        planes(g, ys[g], halves[1], nc.vector.tensor_copy)
+        for q in range(QUADS):
+            nc.scalar.dma_start(
+                out=out_2.bitcast(I32)[:, 4 * q : 4 * q + 4, :],
+                in_=y_s[32 * q : 32 * q + 4 * GROUPS, :].bitcast(I32),
+            )

@@ -22,7 +22,8 @@ PACK = 4
 PASSES = K // (P * PACK)
 GROUPS = N // (P * PACK)
 QUADS = 4
-CHUNKS = (512, 256, 256)
+CHUNKS = (256, 256, 256, 256)
+SQUARED = ()
 
 
 def tile_list_compass_deviation_card_kernel(
@@ -51,6 +52,8 @@ def tile_list_compass_deviation_card_kernel(
         nc.gpsimd.memset(one[:, 0:1], 1.0)
         half_pi = keep.tile([P, 1], F32, name="half_pi")
         nc.vector.tensor_scalar(out=half_pi[:], in0=one[:, 0:1], scalar1=math.pi / 2, scalar2=None, op0=ALU.mult)
+        warm = keep.tile([P, 1], F32, name="warm")
+        nc.scalar.activation(out=warm[:], in_=half_pi[:], func=ACT.Sin)
         w2_s_raw = stage.tile([P, H], U8, name="w2_s_raw", offset=4 * ROOM + 6144 + 64)
         nc.gpsimd.memset(w2_s_raw[:].bitcast(I32), 0)
         w4_s_raw = stage.tile([P, N], U8, name="w4_s_raw", offset=4 * ROOM + 6144 + 576)
@@ -92,28 +95,24 @@ def tile_list_compass_deviation_card_kernel(
         starts = [sum(CHUNKS[:c]) for c in range(len(CHUNKS))]
         v_s, v_w = {}, {}
 
-        def entries(c):
-            return offs_sb[:, starts[c] // 16 : (starts[c] + CHUNKS[c]) // 16]
+        def entries(js):
+            return offs_sb[:, js.start // 16 : js.stop // 16]
 
-        def gather_words(a, c):
-            if a == 0:
-                vw = keep.tile([P, CHUNKS[c]], U32, name=f"v_w{a}{c}", align_bytes=64)
-            else:
-                vw = stage.tile(
-                    [P, CHUNKS[c]], U32, name=f"v_w{a}{c}", align_bytes=64, offset=5 * ROOM + 4096 + 4 * starts[c]
-                )
-            nc.vector.tensor_copy(out=vw[:], in_=tab_w[a][:].bitcast(U32).indirect(entries(c)))
-            v_w[a, c] = vw[:]
+        v_scales = keep.tile([P, S], U8, name="v_scales", align_bytes=64)
+        nc.vector.tensor_copy(out=v_scales[:], in_=tab_s[:].indirect(offs_sb[:]))
+        v_words = [
+            keep.tile([P, S], U32, name="v_words0", align_bytes=64),
+            stage.tile([P, S], U32, name="v_words1", align_bytes=64, offset=5 * ROOM + 4096 + 512),
+        ]
 
-        def gather_scales(c):
-            vs = keep.tile([P, CHUNKS[c]], U8, name=f"v_s{c}", align_bytes=64)
-            nc.vector.tensor_copy(out=vs[:], in_=tab_s[:].indirect(entries(c)))
-            v_s[c] = vs
+        def gather_words(a, js):
+            nc.vector.tensor_copy(out=v_words[a][:, js], in_=tab_w[a][:].bitcast(U32).indirect(entries(js)))
 
-        for c in range(len(CHUNKS)):
-            gather_scales(c)
-        for c in range(len(CHUNKS)):
-            gather_words(0, c)
+        gather_words(0, slice(0, S))
+        for c, width in enumerate(CHUNKS):
+            v_s[c] = v_scales[:, starts[c] : starts[c] + width]
+            for a in range(PASSES):
+                v_w[a, c] = v_words[a][:, starts[c] : starts[c] + width]
 
         w1_w, w1_s = [], []
         for a in range(PASSES):
@@ -132,20 +131,19 @@ def tile_list_compass_deviation_card_kernel(
             w1_w.append(ww)
             w1_s.append(ws)
 
-        gather_words(1, 0)
+        gather_words(1, slice(0, CHUNKS[0]))
 
         w2_w = stage.tile([P, PASSES, H], I32, name="w2_w", align_bytes=64, offset=5 * ROOM)
         nc.vector.tensor_copy(
             out=w2_w[:].rearrange("p a (t m e) -> p a m t e", t=PACK, e=4),
             in_=w2_raw[:].rearrange("p a (m e t) -> p a m t e", t=PACK, e=4),
         )
-        w2_s = stage.tile([P, H], U8, name="w2_s", align_bytes=64, offset=4 * ROOM + 3072)
+        w2_s = stage.tile([P, H], U8, name="w2_s", align_bytes=64, offset=5 * ROOM + 4096)
         nc.vector.tensor_copy(
             out=w2_s[:].rearrange("p (t m) -> p t m", t=PACK),
             in_=w2_s_raw[:].rearrange("p (m t) -> p t m", t=PACK),
         )
-        for c in range(1, len(CHUNKS)):
-            gather_words(1, c)
+        gather_words(1, slice(CHUNKS[0], S))
 
         field_rows = field.rearrange("(g p u t) j -> g u p t j", p=P, u=2, t=2)
         field_sb = {}
@@ -169,44 +167,59 @@ def tile_list_compass_deviation_card_kernel(
 
         g2 = {}
 
-        h_q = []
-        def product(c, t, words, scales):
-            cols = slice(P * t, P * (t + 1))
-            acc = psum.tile([P, CHUNKS[c]], F32, name="first")
-            for a in range(PASSES):
-                nc.tensor.matmul_mx(
-                    out=acc[:],
-                    lhsT=words[a][:, cols].bitcast(FP8X4), lhsT_scale=scales[a][:, cols],
-                    rhs=v_w[a, c].bitcast(FP8X4), rhs_scale=v_s[c][4 * a : P, :],
-                    start=(a == 0), stop=(a == PASSES - 1),
-                )
+        soft_m2 = keep.tile([P, PACK], F32, name="soft_m2")
+        nc.scalar.activation(out=soft_m2[:], in_=soft_sb[:], func=ACT.Copy, scale=-2.0)
+        h_w = keep.tile([P, S], U32, name="h_w", align_bytes=64)
+        h_s = keep.tile([P, S], U8, name="h_s", align_bytes=64)
+        def product(c, pair, words, scales):
+            acc = psum.tile([P, 2, CHUNKS[c]], F32, name="first")
+            for e in range(2):
+                cols = slice(P * (2 * pair + e), P * (2 * pair + e + 1))
+                for a in range(PASSES):
+                    nc.tensor.matmul_mx(
+                        out=acc[:, e, :],
+                        lhsT=words[a][:, cols].bitcast(FP8X4), lhsT_scale=scales[a][:, cols],
+                        rhs=v_w[a, c].bitcast(FP8X4), rhs_scale=v_s[c][4 * a : P, :],
+                        start=(a == 0), stop=(a == PASSES - 1),
+                    )
             return acc
 
-        def cosine(c, t):
-            acc = product(c, t, w1_w, w1_s)
-            abs_a = work.tile([P, CHUNKS[c]], F32, name="abs_a")
-            nc.scalar.activation(out=abs_a[:], in_=acc[:], func=ACT.Abs)
-            cos_a = work.tile([P, CHUNKS[c]], F32, name="cos_a", bufs=4)
-            nc.scalar.activation(out=cos_a[:], in_=abs_a[:], func=ACT.Sin, bias=half_pi[:], scale=-1.0)
-            return cos_a
+        def cosine(c, pair):
+            acc = product(c, pair, w1_w, w1_s)
+            term = work.tile([P, 2, CHUNKS[c]], F32, name="term", bufs=4)
+            inner = work.tile([P, 2, CHUNKS[c]], F32, name="inner", bufs=3)
+            if (c, pair) in SQUARED:
+                nc.scalar.activation(out=inner[:], in_=acc[:], func=ACT.Sin, scale=0.5)
+                for e in range(2):
+                    t = 2 * pair + e
+                    nc.vector.scalar_tensor_tensor(
+                        out=term[:, e, :], in0=inner[:, e, :], scalar=soft_m2[:, t : t + 1], in1=inner[:, e, :],
+                        op0=ALU.mult, op1=ALU.mult,
+                    )
+            else:
+                nc.scalar.activation(out=inner[:], in_=acc[:], func=ACT.Abs)
+                nc.scalar.activation(out=term[:], in_=inner[:], func=ACT.Sin, bias=half_pi[:], scale=-1.0)
+            return term
 
-        def sine(c, t):
-            acc = product(c, t, [w2_w[:, a, :] for a in range(PASSES)], [w2_s[4 * a : P, :] for a in range(PASSES)])
-            sin_b = work.tile([P, CHUNKS[c]], F32, name="sin_b", bufs=4)
+        def sine(c, pair):
+            acc = product(c, pair, [w2_w[:, a, :] for a in range(PASSES)], [w2_s[4 * a : P, :] for a in range(PASSES)])
+            sin_b = work.tile([P, 2, CHUNKS[c]], F32, name="sin_b", bufs=4)
             nc.scalar.activation(out=sin_b[:], in_=acc[:], func=ACT.Sin)
             return sin_b
 
         for c, width in enumerate(CHUNKS):
             u = work.tile([P, PACK, width], F32, name="u")
             if c == 0:
-                early = [cosine(c, t) for t in range(PACK)]
-            for t in range(PACK):
-                cos_a = early[t] if c == 0 else cosine(c, t)
-                sin_b = sine(c, t)
-                nc.vector.scalar_tensor_tensor(
-                    out=u[:, t, :], in0=cos_a[:], scalar=soft_sb[:, t : t + 1], in1=sin_b[:],
-                    op0=ALU.mult, op1=ALU.subtract,
-                )
+                early = [cosine(c, pair) for pair in range(2)]
+            for pair in range(2):
+                term = early[pair] if c == 0 else cosine(c, pair)
+                sin_b = sine(c, pair)
+                for e in range(2):
+                    t = 2 * pair + e
+                    nc.vector.scalar_tensor_tensor(
+                        out=u[:, t, :], in0=term[:, e, :], scalar=soft_sb[:, t : t + 1], in1=sin_b[:, e, :],
+                        op0=(ALU.add if (c, pair) in SQUARED else ALU.mult), op1=ALU.subtract,
+                    )
             h_bf = work.tile([P, width, PACK], BF16, name="h_bf", align_bytes=64)
             nc.vector.tensor_tensor(
                 out=h_bf[:].rearrange("p (c e) t -> p c t e", e=4),
@@ -214,10 +227,10 @@ def tile_list_compass_deviation_card_kernel(
                 in1=gain_sb[:].unsqueeze(1).unsqueeze(3).to_broadcast([P, width // 4, PACK, 4]),
                 op=ALU.mult,
             )
-            h_w = keep.tile([P, width], U32, name=f"h_w{c}", align_bytes=64)
-            h_s = keep.tile([P, width], U8, name=f"h_s{c}", align_bytes=64)
-            nc.vector.quantize_mx(out=h_w[:].bitcast(FP8X4), scales=h_s[:], in_=h_bf[:].rearrange("p j t -> p (j t)"))
-            h_q.append((h_w, h_s))
+            js = slice(starts[c], starts[c] + width)
+            nc.vector.quantize_mx(
+                out=h_w[:, js].bitcast(FP8X4), scales=h_s[:, js], in_=h_bf[:].rearrange("p j t -> p (j t)")
+            )
 
         out_rows = out_0.rearrange("(g p t) m -> g t p m", p=P, t=PACK)
         out_words = out_1.rearrange("g p m t -> g p (m t)").bitcast(I32)
@@ -228,14 +241,15 @@ def tile_list_compass_deviation_card_kernel(
             g2[g, t] = keep.tile([P, S], F32, name=f"g2_{s}", tag=f"ring{s % 3}")
             if s >= 1:
                 sums = work.tile([P, S], F32, name="sums")
-            for c, width in enumerate(CHUNKS):
-                js = slice(starts[c], starts[c] + width)
-                acc = psum.tile([P, width], F32, name=f"second{min(c, 1)}", bufs=2)
+            cuts = (0, 512, 768, 1024) if s == 0 else (0, 512, 1024)
+            for c in range(len(cuts) - 1):
+                js = slice(cuts[c], cuts[c + 1])
+                acc = psum.tile([P, cuts[c + 1] - cuts[c]], F32, name=f"second{min(c, 1)}", bufs=2)
                 nc.tensor.matmul_mx(
                     out=acc[:],
                     lhsT=w4_w[:].bitcast(U8)[:, 2 * P * s : 2 * P * (s + 1)].bitcast(FP4X4),
                     lhsT_scale=w4_s[:, P * s : P * (s + 1)],
-                    rhs=h_q[c][0][:].bitcast(FP8X4), rhs_scale=h_q[c][1][:],
+                    rhs=h_w[:, js].bitcast(FP8X4), rhs_scale=h_s[:, js],
                     start=True, stop=True,
                 )
                 if s >= 1:
@@ -248,8 +262,14 @@ def tile_list_compass_deviation_card_kernel(
         def pick(g, t, y, ms, x):
             cols = slice(ms.start // 16, ms.stop // 16)
             nc.vector.tensor_copy(out=x[:, 0, ms], in_=g2[g, t][:].indirect(pos1_sb[:, cols]))
-            nc.vector.tensor_copy(out=x[:, 1, ms], in_=g2[g, t][:].indirect(pos2_sb[:, cols]))
-            nc.vector.tensor_tensor(out=y[:, t, ms], in0=x[:, 0, ms], in1=x[:, 1, ms], op=ALU.max)
+            mid = (ms.start + ms.stop) // 2
+            parts = (slice(ms.start, mid), slice(mid, ms.stop))
+            for part in parts:
+                nc.vector.tensor_copy(
+                    out=x[:, 1, part], in_=g2[g, t][:].indirect(pos2_sb[:, part.start // 16 : part.stop // 16])
+                )
+            for part in parts:
+                nc.vector.tensor_tensor(out=y[:, t, part], in0=x[:, 0, part], in1=x[:, 1, part], op=ALU.max)
             nc.sync.dma_start(out=out_rows[g, t][:, ms], in_=y[:, t, ms])
 
         def planes(g, y, ms, copy):

@@ -24,6 +24,7 @@ GROUPS = N // (P * PACK)
 QUADS = 4
 CHUNKS = (256, 256, 256, 256)
 SQUARED = ()
+SHARE = 128
 
 
 def tile_list_compass_deviation_card_kernel(
@@ -236,9 +237,11 @@ def tile_list_compass_deviation_card_kernel(
         out_words = out_1.rearrange("g p m t -> g p (m t)").bitcast(I32)
         y_s = keep.tile([P, PAIRS], U8, name="y_s", align_bytes=64)
 
+        ring = ctx.enter_context(tc.tile_pool(name="ring", bufs=1))
+
         def second_stage(g, t):
             s = PACK * g + t
-            g2[g, t] = keep.tile([P, S], F32, name=f"g2_{s}", tag=f"ring{s % 3}")
+            g2[g, t] = ring.tile([P, S], F32, name=f"g2_{s}", offset=4 * S * (s % 3))
             if s >= 1:
                 sums = work.tile([P, S], F32, name="sums")
             cuts = (0, 512, 768, 1024) if s == 0 else (0, 512, 1024)
@@ -252,24 +255,39 @@ def tile_list_compass_deviation_card_kernel(
                     rhs=h_w[:, js].bitcast(FP8X4), rhs_scale=h_s[:, js],
                     start=True, stop=True,
                 )
-                if s >= 1:
-                    nc.scalar.copy(out=sums[:, js], in_=acc[:])
-                else:
-                    nc.vector.tensor_tensor(out=g2[g, t][:, js], in0=acc[:], in1=field_sb[g, t][:, js], op=ALU.mult)
+                cut = js.start if s == 0 else min(js.stop, S - SHARE)
+                if cut > js.start:
+                    nc.scalar.copy(out=sums[:, js.start : cut], in_=acc[:, : cut - js.start])
+                if cut < js.stop:
+                    nc.vector.tensor_tensor(
+                        out=g2[g, t][:, cut : js.stop], in0=acc[:, cut - js.start :],
+                        in1=field_sb[g, t][:, cut : js.stop], op=ALU.mult,
+                    )
             if s >= 1:
-                nc.gpsimd.tensor_tensor(out=g2[g, t][:], in0=sums[:], in1=field_sb[g, t], op=ALU.mult)
-
-        def pick(g, t, y, ms, x):
-            cols = slice(ms.start // 16, ms.stop // 16)
-            nc.vector.tensor_copy(out=x[:, 0, ms], in_=g2[g, t][:].indirect(pos1_sb[:, cols]))
-            mid = (ms.start + ms.stop) // 2
-            parts = (slice(ms.start, mid), slice(mid, ms.stop))
-            for part in parts:
-                nc.vector.tensor_copy(
-                    out=x[:, 1, part], in_=g2[g, t][:].indirect(pos2_sb[:, part.start // 16 : part.stop // 16])
+                nc.gpsimd.tensor_tensor(
+                    out=g2[g, t][:, : S - SHARE], in0=sums[:, : S - SHARE], in1=field_sb[g, t][:, : S - SHARE],
+                    op=ALU.mult,
                 )
-            for part in parts:
-                nc.vector.tensor_tensor(out=y[:, t, part], in0=x[:, 0, part], in1=x[:, 1, part], op=ALU.max)
+
+        def pick(g, t, y, ms):
+            s = PACK * g + t
+            width = ms.stop - ms.start
+            half = width // 2
+            x1 = work.tile([P, width], F32, name="x1")
+            nc.vector.tensor_copy(out=x1[:], in_=g2[g, t][:].indirect(pos1_sb[:, ms.start // 16 : ms.stop // 16]))
+            if s + 2 < PACK * GROUPS:
+                x2a = ring.tile([P, half], F32, name=f"x2a_{s}", offset=4 * S * ((s + 2) % 3))
+            else:
+                x2a = work.tile([P, half], F32, name="x2a")
+            x2b = work.tile([P, half], F32, name="x2b")
+            parts = ((x2a, 0), (x2b, half))
+            for x2, at in parts:
+                first = (ms.start + at) // 16
+                nc.vector.tensor_copy(out=x2[:], in_=g2[g, t][:].indirect(pos2_sb[:, first : first + half // 16]))
+            for x2, at in parts:
+                nc.vector.tensor_tensor(
+                    out=y[:, t, ms.start + at : ms.start + at + half], in0=x1[:, at : at + half], in1=x2[:], op=ALU.max
+                )
             nc.sync.dma_start(out=out_rows[g, t][:, ms], in_=y[:, t, ms])
 
         def planes(g, y, ms, copy):
@@ -279,7 +297,10 @@ def tile_list_compass_deviation_card_kernel(
                 out=y_bf[:].rearrange("p (c e) t -> p c t e", e=4),
                 in_=y[:, :, ms].rearrange("p t (c e) -> p c t e", e=4),
             )
-            y_w = work.tile([P, width], I32, name="y_w", align_bytes=64)
+            if g == 0:
+                y_w = ring.tile([P, width], I32, name="y_w0", align_bytes=64, offset=2048)
+            else:
+                y_w = work.tile([P, width], I32, name="y_w", align_bytes=64)
             nc.vector.quantize_mx(
                 out=y_w[:].bitcast(FP8X4), scales=y_s[4 * g : P, ms], in_=y_bf[:].rearrange("p m t -> p (m t)")
             )
@@ -292,10 +313,9 @@ def tile_list_compass_deviation_card_kernel(
         second_stage(*slices[0])
         second_stage(*slices[1])
         for i, (g, t) in enumerate(slices):
-            x = keep.tile([P, 2, PAIRS], F32, name=f"x{i}", tag=f"ring{(i + 2) % 3}")
             for ms in (halves if i == len(slices) - 1 else (whole,)):
-                pick(g, t, ys[g], ms, x)
-            if (g, t) == (1, 0):
+                pick(g, t, ys[g], ms)
+            if (g, t) == (1, 2):
                 planes(0, ys[0], whole, nc.scalar.copy)
             if i + 2 < len(slices):
                 second_stage(*slices[i + 2])

import math
from contextlib import ExitStack

import concourse.mybir as mybir

K, T, S, H, N, PAIRS = 1024, 2048, 1024, 512, 1024, 512
FLOPS = 2 * (2 * K * H * S + H * N * S)

F32 = mybir.dt.float32
BF16 = mybir.dt.bfloat16
I32 = mybir.dt.int32
U32 = mybir.dt.uint32
U16 = mybir.dt.uint16
U8 = mybir.dt.uint8
FP8X4 = mybir.dt.float8_e4m3fn_x4
FP4X4 = mybir.dt.float4_e2m1fn_x4
ALU = mybir.AluOpType
ACT = mybir.ActivationFunctionType

P = 128
PACK = 4
PASSES = K // (P * PACK)
GROUPS = N // (P * PACK)
QUADS = 4
CHUNKS = (256, 256, 256, 256)
SQUARED = ()
SHARE = 128


def tile_list_compass_deviation_card_kernel(
    tc, tab_words, tab_scales, offs, pos1, pos2, w1, w2_words, w2_scales, soft, gain,
    w4_words, w4_scales, field, out_0, out_1, out_2,
):
    nc = tc.nc
    with ExitStack() as ctx:
        keep = ctx.enter_context(tc.tile_pool(name="keep", bufs=1))
        work = ctx.enter_context(tc.tile_pool(name="work", bufs=2))
        psum = ctx.enter_context(tc.psum_pool(name="psum", bufs=4))

        def load_scale_rows(queue, tile, scales):
            planes = scales.shape[0]
            for q in range(QUADS):
                queue.dma_start(
                    out=tile[32 * q : 32 * q + 4 * planes, :].bitcast(I32),
                    in_=scales.bitcast(I32)[:, 4 * q : 4 * q + 4, :],
                )

        stage = ctx.enter_context(tc.tile_pool(name="stage", bufs=1))
        ROOM = 8192
        tab_s = keep.tile([P, T], U8, name="tab_s", align_bytes=64)
        nc.gpsimd.memset(tab_s[:].bitcast(I32), 0)
        one = stage.tile([P, ROOM], F32, name="one", offset=ROOM)
        nc.gpsimd.memset(one[:, 0:1], 1.0)
        half_pi = keep.tile([P, 1], F32, name="half_pi")
        nc.vector.tensor_scalar(out=half_pi[:], in0=one[:, 0:1], scalar1=math.pi / 2, scalar2=None, op0=ALU.mult)
        warm = keep.tile([P, 1], F32, name="warm")
        nc.scalar.activation(out=warm[:], in_=half_pi[:], func=ACT.Sin)
        w2_s_raw = stage.tile([P, H], U8, name="w2_s_raw", offset=4 * ROOM + 6144 + 64)
        nc.gpsimd.memset(w2_s_raw[:].bitcast(I32), 0)
        w4_s_raw = stage.tile([P, N], U8, name="w4_s_raw", offset=4 * ROOM + 6144 + 576)
        nc.gpsimd.memset(w4_s_raw[:].bitcast(I32), 0)

        tab_w = [stage.tile([P, T], I32, name=f"tab_w{a}", offset=a * ROOM) for a in range(PASSES)]
        w1_raw = [stage.tile([P, PACK, H], F32, name=f"w1_raw{a}", offset=(2 + a) * ROOM) for a in range(PASSES)]
        w2_raw = stage.tile([P, PASSES, H], I32, name="w2_raw", offset=4 * ROOM)
        w4_raw = stage.tile([P, N // 2], I32, name="w4_raw", offset=4 * ROOM + 4096)
        soft_sb = stage.tile([P, PACK], F32, name="soft_sb", offset=4 * ROOM + 6144)
        gain_sb = stage.tile([P, PACK], F32, name="gain_sb", offset=4 * ROOM + 6144 + 32)

        def load_tab(a):
            nc.sync.dma_start(out=tab_w[a][:], in_=tab_words[a].rearrange("p t i -> p (t i)").bitcast(I32))

        def load_w1(a):
            nc.sync.dma_start(
                out=w1_raw[a][:], in_=w1[512 * a : 512 * (a + 1), :].rearrange("(p i) r -> p i r", i=PACK)
            )

        offs_sb = keep.tile([P, S // 16], U16, name="offs_sb")
        nc.sync.dma_start(out=offs_sb[:], in_=offs)
        load_tab(0)
        pos1_sb = keep.tile([P, PAIRS // 16], U16, name="pos1_sb")
        nc.sync.dma_start(out=pos1_sb[:], in_=pos1)
        pos2_sb = keep.tile([P, PAIRS // 16], U16, name="pos2_sb")
        nc.sync.dma_start(out=pos2_sb[:], in_=pos2)
        load_scale_rows(nc.scalar, tab_s, tab_scales)
        load_w1(0)
        load_w1(1)
        load_tab(1)
        nc.sync.dma_start(out=w2_raw[:], in_=w2_words.rearrange("a p c i -> p a (c i)").bitcast(I32))
        load_scale_rows(nc.sync, w2_s_raw, w2_scales)
        nc.sync.dma_start(out=soft_sb[:], in_=soft.rearrange("(p t) -> p t", t=PACK))
        nc.sync.dma_start(out=gain_sb[:], in_=gain.rearrange("(p t) -> p t", t=PACK))
        nc.sync.dma_start(out=w4_raw[:], in_=w4_words[0].bitcast(I32))
        load_scale_rows(nc.sync, w4_s_raw, w4_scales)

        starts = [sum(CHUNKS[:c]) for c in range(len(CHUNKS))]
        v_s, v_w = {}, {}

        def entries(js):
            return offs_sb[:, js.start // 16 : js.stop // 16]

        v_scales = keep.tile([P, S], U8, name="v_scales", align_bytes=64)
        nc.vector.tensor_copy(out=v_scales[:], in_=tab_s[:].indirect(offs_sb[:]))
        v_words = [
            keep.tile([P, S], U32, name="v_words0", align_bytes=64),
            stage.tile([P, S], U32, name="v_words1", align_bytes=64, offset=5 * ROOM + 4096 + 512),
        ]

        def gather_words(a, js):
            nc.vector.tensor_copy(out=v_words[a][:, js], in_=tab_w[a][:].bitcast(U32).indirect(entries(js)))

        gather_words(0, slice(0, S))
        for c, width in enumerate(CHUNKS):
            v_s[c] = v_scales[:, starts[c] : starts[c] + width]
            for a in range(PASSES):
                v_w[a, c] = v_words[a][:, starts[c] : starts[c] + width]

        w1_w, w1_s = [], []
        for a in range(PASSES):
            if a == 0:
                wb = keep.tile([P, H * PACK], BF16, name=f"w1_bf{a}", align_bytes=64)
            else:
                wb = stage.tile([P, H * PACK], BF16, name=f"w1_bf{a}", align_bytes=64, offset=5 * ROOM + 4096 - 64)
            for ms, copy in ((slice(0, P // 2), nc.scalar.copy), (slice(P // 2, P), nc.vector.tensor_copy)):
                copy(
                    out=wb[:].rearrange("p (t m i) -> p m i t", t=PACK, i=PACK)[:, ms],
                    in_=w1_raw[a][:].rearrange("p i (m t) -> p m i t", t=PACK)[:, ms],
                )
            ww = keep.tile([P, H], U32, name=f"w1_w{a}", align_bytes=64)
            ws = keep.tile([P, H], U8, name=f"w1_s{a}", align_bytes=64)
            nc.vector.quantize_mx(out=ww[:].bitcast(FP8X4), scales=ws[:], in_=wb[:])
            w1_w.append(ww)
            w1_s.append(ws)

        gather_words(1, slice(0, CHUNKS[0]))

        w2_w = stage.tile([P, PASSES, H], I32, name="w2_w", align_bytes=64, offset=5 * ROOM)
        nc.vector.tensor_copy(
            out=w2_w[:].rearrange("p a (t m e) -> p a m t e", t=PACK, e=4),
            in_=w2_raw[:].rearrange("p a (m e t) -> p a m t e", t=PACK, e=4),
        )
        w2_s = stage.tile([P, H], U8, name="w2_s", align_bytes=64, offset=5 * ROOM + 4096)
        nc.vector.tensor_copy(
            out=w2_s[:].rearrange("p (t m) -> p t m", t=PACK),
            in_=w2_s_raw[:].rearrange("p (m t) -> p t m", t=PACK),
        )
        gather_words(1, slice(CHUNKS[0], S))

        field_rows = field.rearrange("(g p u t) j -> g u p t j", p=P, u=2, t=2)
        field_sb = {}
        for k, room in enumerate((0, 2, 3, 1)):
            g, pair = divmod(k, 2)
            f = stage.tile([P, 2, S], F32, name=f"field{k}", offset=room * ROOM)
            nc.sync.dma_start(out=f[:], in_=field_rows[g, pair])
            for t in range(2):
                field_sb[g, 2 * pair + t] = f[:, t, :]

        w4_w = stage.tile([P, N // 2], I32, name="w4_w", align_bytes=64, offset=4 * ROOM)
        nc.vector.tensor_copy(
            out=w4_w[:].bitcast(U16).rearrange("p (g t m) -> p g t m", g=GROUPS, t=PACK),
            in_=w4_raw[:].bitcast(U16).rearrange("p (g m t) -> p g t m", g=GROUPS, t=PACK),
        )
        w4_s = stage.tile([P, N], U8, name="w4_s", align_bytes=64, offset=4 * ROOM + 2048)
        nc.vector.tensor_copy(
            out=w4_s[:].rearrange("p (g t m) -> p g t m", g=GROUPS, t=PACK),
            in_=w4_s_raw[:].rearrange("p (g m t) -> p g t m", g=GROUPS, t=PACK),
        )

        g2 = {}

        soft_m2 = keep.tile([P, PACK], F32, name="soft_m2")
        nc.scalar.activation(out=soft_m2[:], in_=soft_sb[:], func=ACT.Copy, scale=-2.0)
        h_w = keep.tile([P, S], U32, name="h_w", align_bytes=64)
        h_s = keep.tile([P, S], U8, name="h_s", align_bytes=64)
        def product(c, pair, words, scales):
            acc = psum.tile([P, 2, CHUNKS[c]], F32, name="first")
            for e in range(2):
                cols = slice(P * (2 * pair + e), P * (2 * pair + e + 1))
                for a in range(PASSES):
                    nc.tensor.matmul_mx(
                        out=acc[:, e, :],
                        lhsT=words[a][:, cols].bitcast(FP8X4), lhsT_scale=scales[a][:, cols],
                        rhs=v_w[a, c].bitcast(FP8X4), rhs_scale=v_s[c][4 * a : P, :],
                        start=(a == 0), stop=(a == PASSES - 1),
                    )
            return acc

        def cosine(c, pair):
            acc = product(c, pair, w1_w, w1_s)
            term = work.tile([P, 2, CHUNKS[c]], F32, name="term", bufs=4)
            inner = work.tile([P, 2, CHUNKS[c]], F32, name="inner", bufs=3)
            if (c, pair) in SQUARED:
                nc.scalar.activation(out=inner[:], in_=acc[:], func=ACT.Sin, scale=0.5)
                for e in range(2):
                    t = 2 * pair + e
                    nc.vector.scalar_tensor_tensor(
                        out=term[:, e, :], in0=inner[:, e, :], scalar=soft_m2[:, t : t + 1], in1=inner[:, e, :],
                        op0=ALU.mult, op1=ALU.mult,
                    )
            else:
                nc.scalar.activation(out=inner[:], in_=acc[:], func=ACT.Abs)
                nc.scalar.activation(out=term[:], in_=inner[:], func=ACT.Sin, bias=half_pi[:], scale=-1.0)
            return term

        def sine(c, pair):
            acc = product(c, pair, [w2_w[:, a, :] for a in range(PASSES)], [w2_s[4 * a : P, :] for a in range(PASSES)])
            sin_b = work.tile([P, 2, CHUNKS[c]], F32, name="sin_b", bufs=4)
            nc.scalar.activation(out=sin_b[:], in_=acc[:], func=ACT.Sin)
            return sin_b

        for c, width in enumerate(CHUNKS):
            u = work.tile([P, PACK, width], F32, name="u")
            if c == 0:
                early = [cosine(c, pair) for pair in range(2)]
            for pair in range(2):
                term = early[pair] if c == 0 else cosine(c, pair)
                sin_b = sine(c, pair)
                for e in range(2):
                    t = 2 * pair + e
                    nc.vector.scalar_tensor_tensor(
                        out=u[:, t, :], in0=term[:, e, :], scalar=soft_sb[:, t : t + 1], in1=sin_b[:, e, :],
                        op0=(ALU.add if (c, pair) in SQUARED else ALU.mult), op1=ALU.subtract,
                    )
            h_bf = work.tile([P, width, PACK], BF16, name="h_bf", align_bytes=64)
            nc.vector.tensor_tensor(
                out=h_bf[:].rearrange("p (c e) t -> p c t e", e=4),
                in0=u[:].rearrange("p t (c e) -> p c t e", e=4),
                in1=gain_sb[:].unsqueeze(1).unsqueeze(3).to_broadcast([P, width // 4, PACK, 4]),
                op=ALU.mult,
            )
            js = slice(starts[c], starts[c] + width)
            nc.vector.quantize_mx(
                out=h_w[:, js].bitcast(FP8X4), scales=h_s[:, js], in_=h_bf[:].rearrange("p j t -> p (j t)")
            )

        out_rows = out_0.rearrange("(g p t) m -> g t p m", p=P, t=PACK)
        out_words = out_1.rearrange("g p m t -> g p (m t)").bitcast(I32)
        y_s = keep.tile([P, PAIRS], U8, name="y_s", align_bytes=64)

        ring = ctx.enter_context(tc.tile_pool(name="ring", bufs=1))

        def second_stage(g, t):
            s = PACK * g + t
            g2[g, t] = ring.tile([P, S], F32, name=f"g2_{s}", offset=4 * S * (s % 3))
            if s >= 1:
                sums = work.tile([P, S], F32, name="sums")
            cuts = (0, 512, 768, 1024) if s == 0 else (0, 512, 1024)
            for c in range(len(cuts) - 1):
                js = slice(cuts[c], cuts[c + 1])
                acc = psum.tile([P, cuts[c + 1] - cuts[c]], F32, name=f"second{min(c, 1)}", bufs=2)
                nc.tensor.matmul_mx(
                    out=acc[:],
                    lhsT=w4_w[:].bitcast(U8)[:, 2 * P * s : 2 * P * (s + 1)].bitcast(FP4X4),
                    lhsT_scale=w4_s[:, P * s : P * (s + 1)],
                    rhs=h_w[:, js].bitcast(FP8X4), rhs_scale=h_s[:, js],
                    start=True, stop=True,
                )
                cut = js.start if s == 0 else min(js.stop, S - SHARE)
                if cut > js.start:
                    nc.scalar.copy(out=sums[:, js.start : cut], in_=acc[:, : cut - js.start])
                if cut < js.stop:
                    nc.vector.tensor_tensor(
                        out=g2[g, t][:, cut : js.stop], in0=acc[:, cut - js.start :],
                        in1=field_sb[g, t][:, cut : js.stop], op=ALU.mult,
                    )
            if s >= 1:
                nc.gpsimd.tensor_tensor(
                    out=g2[g, t][:, : S - SHARE], in0=sums[:, : S - SHARE], in1=field_sb[g, t][:, : S - SHARE],
                    op=ALU.mult,
                )

        def pick(g, t, y, ms):
            s = PACK * g + t
            width = ms.stop - ms.start
            half = width // 2
            x1 = work.tile([P, width], F32, name="x1")
            nc.vector.tensor_copy(out=x1[:], in_=g2[g, t][:].indirect(pos1_sb[:, ms.start // 16 : ms.stop // 16]))
            if s + 2 < PACK * GROUPS:
                x2a = ring.tile([P, half], F32, name=f"x2a_{s}", offset=4 * S * ((s + 2) % 3))
            else:
                x2a = work.tile([P, half], F32, name="x2a")
            x2b = work.tile([P, half], F32, name="x2b")
            parts = ((x2a, 0), (x2b, half))
            for x2, at in parts:
                first = (ms.start + at) // 16
                nc.vector.tensor_copy(out=x2[:], in_=g2[g, t][:].indirect(pos2_sb[:, first : first + half // 16]))
            for x2, at in parts:
                nc.vector.tensor_tensor(
                    out=y[:, t, ms.start + at : ms.start + at + half], in0=x1[:, at : at + half], in1=x2[:], op=ALU.max
                )
            nc.sync.dma_start(out=out_rows[g, t][:, ms], in_=y[:, t, ms])

        def planes(g, y, ms, copy):
            width = ms.stop - ms.start
            y_bf = work.tile([P, width, PACK], BF16, name="y_bf", align_bytes=64)
            copy(
                out=y_bf[:].rearrange("p (c e) t -> p c t e", e=4),
                in_=y[:, :, ms].rearrange("p t (c e) -> p c t e", e=4),
            )
            if g == 0:
                y_w = ring.tile([P, width], I32, name="y_w0", align_bytes=64, offset=2048)
            else:
                y_w = work.tile([P, width], I32, name="y_w", align_bytes=64)
            nc.vector.quantize_mx(
                out=y_w[:].bitcast(FP8X4), scales=y_s[4 * g : P, ms], in_=y_bf[:].rearrange("p m t -> p (m t)")
            )
            nc.sync.dma_start(out=out_words[g][:, ms], in_=y_w[:])

        whole = slice(0, PAIRS)
        halves = (slice(0, PAIRS // 2), slice(PAIRS // 2, PAIRS))
        ys = [keep.tile([P, PACK, PAIRS], F32, name=f"y{g}") for g in range(GROUPS)]
        slices = [(g, t) for g in range(GROUPS) for t in range(PACK)]
        second_stage(*slices[0])
        second_stage(*slices[1])
        for i, (g, t) in enumerate(slices):
            for ms in (halves if i == len(slices) - 1 else (whole,)):
                pick(g, t, ys[g], ms)
            if (g, t) == (1, 2):
                planes(0, ys[0], whole, nc.scalar.copy)
            if i + 2 < len(slices):
                second_stage(*slices[i + 2])
        planes(g, ys[g], halves[0], nc.scalar.copy)
        planes(g, ys[g], halves[1], nc.vector.tensor_copy)
        for q in range(QUADS):
            nc.scalar.dma_start(
                out=out_2.bitcast(I32)[:, 4 * q : 4 * q + 4, :],
                in_=y_s[32 * q : 32 * q + 4 * GROUPS, :].bitcast(I32),
            )
